import numpy as np
import ml_dtypes


def mxq(x, axis, fmt="e4m3"):
    dtype, down = {"e4m3": (ml_dtypes.float8_e4m3fn, 7), "e5m2": (ml_dtypes.float8_e5m2, 14)}[fmt]
    v = np.moveaxis(np.asarray(x, np.float32).astype(ml_dtypes.bfloat16).astype(np.float64), axis, -1)
    blocks = v.reshape(v.shape[:-1] + (-1, 32))
    amax = np.abs(blocks).max(-1, keepdims=True)
    byte = np.maximum(np.where(amax > 0, np.frexp(amax)[1] - 1 + 127, 0) - down, 1)
    scale = np.exp2(byte - 127.0)
    codes = (blocks / scale).astype(np.float32).astype(dtype).astype(np.float64)
    return np.moveaxis((codes * scale).reshape(v.shape), -1, axis)


WIDE = False


def mx_kscale(k):
    if not WIDE:
        return np.ones(k)
    levels = np.array([10, -10, 5, -5, 0])
    if k % 512:
        return np.exp2(np.random.permutation(np.resize(levels, k // 32))).repeat(32)
    a = np.empty((k // 512, 16))
    for p in range(k // 512):
        a[p, :8] = np.random.permutation(np.resize(levels, 8))
        for g in range(8):
            far = levels[np.abs(levels - a[p, g]) >= 10]
            a[p, g + 8] = far[np.random.randint(len(far))]
    return np.exp2(a.ravel()).repeat(32)


def f64(x):
    return np.asarray(x).astype(np.float64)


def striped(idx):
    return np.tile(idx.reshape(-1, 16).T, (8, 1)).astype(np.uint16)


def unstriped(offs):
    return offs[:16].T.reshape(-1).astype(np.int64)


E2M1 = np.array([0.0, 0.5, 1.0, 1.5, 2.0, 3.0, 4.0, 6.0, -0.0, -0.5, -1.0, -1.5, -2.0, -3.0, -4.0, -6.0])


def pack_weight(w, fmt):
    k, n = w.shape
    w = f64(np.asarray(w, np.float32).astype(ml_dtypes.bfloat16)).reshape(k // 32, 32, n)
    amax = np.abs(w).max(1)
    if fmt == "e4m3":
        byte = np.frexp(amax)[1] - 1 + 127 - 7
    else:
        mant, ex = np.frexp(amax / 6.0)
        byte = np.where(mant > 0.5, ex, ex - 1) + 127
    byte = np.clip(np.where(amax > 0, byte, 1), 1, 254)
    scaled = (w * np.exp2(127.0 - byte)[:, None, :]).reshape(k, n).astype(np.float32)
    by_word = np.ascontiguousarray(scaled.reshape(k // 512, 128, 4, n).transpose(0, 1, 3, 2))
    if fmt == "e4m3":
        words = by_word.astype(ml_dtypes.float8_e4m3fn).view(np.uint8)
    else:
        c = by_word.astype(ml_dtypes.float4_e2m1fn).view(np.uint8) & 0xF
        words = (c[..., 0::2] | (c[..., 1::2] << 4)).reshape(k // 512, 128, 2 * n)
    return np.ascontiguousarray(words), np.ascontiguousarray(byte.astype(np.uint8).reshape(k // 512, 16, n))


def unpack_weight(words, scales, fmt):
    g, _, n = scales.shape
    words = np.ascontiguousarray(words).reshape(g, 128, n, -1)
    if fmt == "e4m3":
        vals = words.view(ml_dtypes.float8_e4m3fn).astype(np.float64)
    else:
        nib = np.empty((g, 128, n, 4), np.uint8)
        nib[..., 0::2] = words & 0xF
        nib[..., 1::2] = words >> 4
        vals = E2M1[nib]
    vals = vals * np.repeat(np.exp2(scales.astype(np.float64) - 127.0), 8, axis=1)[..., None]
    return vals.transpose(0, 1, 3, 2).reshape(g * 512, n)


K, T, E, C, N = 512, 1536, 12, 128, 384


def by_expert(wq, xq):
    return np.concatenate([wq[e].T @ xq[:, e * C:(e + 1) * C] for e in range(E)], axis=1)


def setup_inputs():
    n = np.random.standard_normal
    s = mx_kscale(K)[:, None]
    w = [pack_weight(m, "e2m1") for m in n((E, K, N)) / np.sqrt(K) / s[None]]
    return {
        "xT": (n((K, T)) * s).astype(np.float32),
        "w_words": np.stack([m[0] for m in w]),
        "w_scales": np.stack([m[1] for m in w]),
        "gate": np.tile(np.random.uniform(0.2, 1.0, E * C), (K, 1)).astype(np.float32),
        "offs": striped(np.random.permutation(T)[:E * C]),
    }


def reference(xT, w_words, w_scales, gate, offs):
    idx = unstriped(offs)
    w = np.stack([unpack_weight(w_words[e], w_scales[e], "e2m1") for e in range(E)])
    xq = mxq(f64(gate) * f64(xT)[:, idx], 0, "e4m3")
    y = by_expert(w, xq)
    out = np.zeros((N, T))
    out[:, idx] = y
    return out

@@ -1,0 +1,197 @@
+from contextlib import ExitStack
+
+import concourse.mybir as mybir
+from concourse.masks import make_identity
+
+K, T, E, C, N = 512, 1536, 12, 128, 384
+FLOPS = 2 * K * N * E * C
+BYTES = 4 * K * T + E * 128 * 2 * N + E * 16 * N + 4 * T + 2 * T * 8 + 4 * N * T
+
+F32 = mybir.dt.float32
+BF16 = mybir.dt.bfloat16
+I32 = mybir.dt.int32
+U32 = mybir.dt.uint32
+U16 = mybir.dt.uint16
+U8 = mybir.dt.uint8
+FP8X4 = mybir.dt.float8_e4m3fn_x4
+FP4X4 = mybir.dt.float4_e2m1fn_x4
+COPY = mybir.ActivationFunctionType.Copy
+
+P = 128
+PACK = 4
+BLOCKS = N // P
+LIST_ROWS = 16
+
+
+def tile_moe_pre_lin_none_kernel(tc, xT, w_words, w_scales, gate, offs, out):
+    nc = tc.nc
+    with ExitStack() as ctx:
+        sb = ctx.enter_context(tc.tile_pool(name="sb", bufs=1))
+        ps = ctx.enter_context(tc.psum_pool(name="ps", bufs=1))
+
+        def bank(index, shape):
+            return ps.tile(shape, F32, name="bank%d" % index)
+
+        gate_rows = sb.tile([P, 3 * C], F32, name="gate_rows")
+        nc.gpsimd.memset(gate_rows[:], 0.0)
+        nc.scalar.dma_start(gate_rows[0:4, :], gate[0, :].rearrange("(j c) -> j c", j=4))
+        ident = sb.tile([P, P], F32, name="ident")
+        make_identity(nc, ident[:])
+
+        offsets = sb.tile([P, T // LIST_ROWS], U16, name="offsets")
+        nc.sync.dma_start(offsets[:], offs)
+
+        def slots_list(e0, e1):
+            return offsets[:, e0 * C // LIST_ROWS : e1 * C // LIST_ROWS]
+
+        x_rows = xT.rearrange("(p t) n -> p t n", t=PACK)
+        planes = []
+        for t in range(PACK):
+            plane = sb.tile([P, T], F32, name="plane%d" % t)
+            nc.sync.dma_start(plane[:], x_rows[:, t, :])
+            planes.append(plane)
+
+        groups = ((0, 2), (2, 6), (6, 12))
+        w_src = w_words.rearrange("e a p b -> p (e a) b").bitcast(I32)
+        s_src = w_scales.rearrange("e a (q r) n -> r q (e a) n", r=4).bitcast(I32)
+        w_tiles = []
+        s_tiles = []
+        for i, (e0, e1) in enumerate(groups):
+            w_tile = sb.tile([P, (e1 - e0) * 2 * N], U8, name="w%d" % i, align_bytes=64)
+            nc.sync.dma_start(w_tile[:].bitcast(I32).rearrange("p (e b) -> p e b", e=e1 - e0), w_src[:, e0:e1, :])
+            w_tiles.append(w_tile)
+            s_tile = sb.tile([P, (e1 - e0) * N], U8, name="s%d" % i, align_bytes=64)
+            nc.vector.memset(s_tile[:].bitcast(I32), 0)
+            for r in range(4):
+                nc.sync.dma_start(
+                    s_tile[:].bitcast(I32).rearrange("p (e n) -> p e n", e=e1 - e0)[r:P:32], s_src[r][:, e0:e1, :]
+                )
+            s_tiles.append(s_tile)
+
+        gate_t = bank(5, [P, 3, P])
+        for i in range(3):
+            nc.tensor.transpose(gate_t[:, i, :], gate_rows[:, i * C : (i + 1) * C], ident[:])
+        gate_col = sb.tile([P, 4, 3], F32, name="gate_col")
+        nc.scalar.activation(gate_col[:], gate_t[:, :, 0:4].rearrange("s i j -> s j i"), COPY)
+
+        gathered = {}
+
+        def gather(group, t, dst):
+            e0, e1 = groups[group]
+            nc.vector.tensor_copy(dst, planes[t][:].indirect(slots_list(e0, e1)))
+            gathered[group, t] = dst
+
+        def scale_by_gate(group, e):
+            e0 = groups[group][0]
+            turned = bank((0, 1, 2)[e % 3] if e < 6 else (0, 1, 3)[e % 3], [P, PACK, P])
+            for t in range(PACK):
+                nc.tensor.transpose(turned[:, t, :], gathered[group, t][:, (e - e0) * C : (e - e0 + 1) * C], ident[:])
+            rounded = sb.tile([P, PACK * P], BF16, name="rounded", bufs=4)
+            nc.scalar.activation(
+                rounded[:].rearrange("s (u p h) -> s u p h", u=2, h=2),
+                turned[:].rearrange("s (u h) p -> s u p h", h=2),
+                COPY,
+                scale=gate_col[:, e // 3, e % 3 : e % 3 + 1],
+            )
+            return rounded
+
+        def prepare_pair(group, pair, dst):
+            e0 = groups[group][0]
+            back = bank((3, 4, 3, 4, 7, 4)[pair], [P, 2, 2, P])
+            for i in range(2):
+                words = scale_by_gate(group, 2 * pair + i)[:].bitcast(F32)
+                for u in range(2):
+                    nc.tensor.transpose(back[:, i, u, :], words[:, u * P : (u + 1) * P], ident[:])
+            first = (2 * pair - e0) * C * 2
+            nc.scalar.copy(
+                dst[:].bitcast(F32)[:, first : first + 4 * C].rearrange("p (i s u) -> p i s u", i=2, u=2),
+                back[:].rearrange("p i u s -> p i s u"),
+            )
+
+        codes = {}
+
+        def quantize(group, src):
+            e0, e1 = groups[group]
+            width = (e1 - e0) * C
+            words = sb.tile([P, width], U32, name="codes%d" % group, align_bytes=64)
+            scales = sb.tile([P, width], U8, name="scales%d" % group, align_bytes=64)
+            for c0 in range(0, width, 512):
+                c1 = min(c0 + 512, width)
+                nc.vector.quantize_mx(
+                    out=words[:, c0:c1].bitcast(FP8X4), scales=scales[:, c0:c1], in_=src[:, PACK * c0 : PACK * c1]
+                )
+            codes[group] = (words, scales)
+
+        results = {}
+
+        def multiply(group, b, banks):
+            e0, e1 = groups[group]
+            words, scales = codes[group]
+            y = sb.tile([P, (e1 - e0) * C], F32, name="y%d_%d" % (group, b))
+            for index, first in zip(banks, range(e0, e1, 4)):
+                last = min(first + 4, e1)
+                acc = bank(index, [P, (last - first) * C])
+                for e in range(first, last):
+                    cols = slice((e - e0) * C, (e - e0 + 1) * C)
+                    w0 = (e - e0) * 2 * N + b * 2 * P
+                    s0 = (e - e0) * N + b * P
+                    nc.tensor.matmul_mx(
+                        out=acc[:, (e - first) * C : (e - first + 1) * C],
+                        lhsT=w_tiles[group][:, w0 : w0 + 2 * P].bitcast(FP4X4),
+                        lhsT_scale=s_tiles[group][:, s0 : s0 + P],
+                        rhs=words[:, cols].bitcast(FP8X4),
+                        rhs_scale=scales[:, cols],
+                        start=True,
+                        stop=True,
+                    )
+                nc.scalar.copy(y[:, (first - e0) * C : (last - e0) * C], acc[:])
+            results[group, b] = y
+
+        windows = [sb.tile([P, T], F32, name="window%d" % b) for b in range(BLOCKS)]
+
+        def scatter(group, b):
+            e0, e1 = groups[group]
+            nc.vector.tensor_copy(windows[b][:].indirect(slots_list(e0, e1)), results[group, b][:])
+
+        g_a = sb.tile([P, PACK, 2 * C], F32, name="g_a", tag="hold_a", align_bytes=64)
+        g_b = sb.tile([P, PACK, 4 * C], F32, name="g_b")
+        g_c0 = sb.tile([P, 6 * C], F32, name="g_c0")
+        for t in range(PACK):
+            gather(0, t, g_a[:, t, :])
+            gather(1, t, g_b[:, t, :])
+            if t == 0:
+                gather(2, 0, g_c0[:])
+
+        q_a = sb.tile([P, 2 * C * PACK], BF16, name="q_a", tag="hold_q", align_bytes=64)
+        prepare_pair(0, 0, q_a)
+        g_c12 = sb.tile([P, 2, 6 * C], F32, name="g_c12", tag="hold_a", align_bytes=64)
+        gather(2, 1, g_c12[:, 0, :])
+        gather(2, 2, g_c12[:, 1, :])
+        quantize(0, q_a)
+        g_c3 = sb.tile([P, 6 * C], F32, name="g_c3", tag="hold_q", align_bytes=64)
+        gather(2, 3, g_c3[:])
+
+        q_b = sb.tile([P, 4 * C * PACK], BF16, name="q_b", align_bytes=64)
+        prepare_pair(1, 1, q_b)
+        multiply(0, 0, [0])
+        scatter(0, 0)
+        prepare_pair(1, 2, q_b)
+        multiply(0, 1, [1])
+        scatter(0, 1)
+        quantize(1, q_b)
+        multiply(0, 2, [3])
+        scatter(0, 2)
+        multiply(1, 0, [5])
+        multiply(1, 2, [6])
+        scatter(1, 0)
+        scatter(1, 2)
+        q_c = sb.tile([P, 6 * C * PACK], BF16, name="q_c", align_bytes=64)
+        for pair in range(3, 6):
+            prepare_pair(2, pair, q_c)
+        quantize(2, q_c)
+        multiply(1, 1, [4])
+        scatter(1, 1)
+        for b in range(BLOCKS):
+            multiply(2, b, [(2, 5), (6, 7), (0, 1)][b])
+            scatter(2, b)
+            nc.sync.dma_start(out[b * P : (b + 1) * P, :], windows[b][:])

@@ -32,9 +32,8 @@ def tile_moe_pre_lin_none_kernel(tc, xT, w_words, w_scales, gate, offs, out):
         def bank(index, shape):
             return ps.tile(shape, F32, name="bank%d" % index)
 
-        gate_rows = sb.tile([P, 3 * C], F32, name="gate_rows")
+        gate_rows = sb.tile([P, C], F32, name="gate_rows")
         nc.gpsimd.memset(gate_rows[:], 0.0)
-        nc.scalar.dma_start(gate_rows[0:4, :], gate[0, :].rearrange("(j c) -> j c", j=4))
         ident = sb.tile([P, P], F32, name="ident")
         make_identity(nc, ident[:])
 
@@ -50,6 +49,8 @@ def tile_moe_pre_lin_none_kernel(tc, xT, w_words, w_scales, gate, offs, out):
             plane = sb.tile([P, T], F32, name="plane%d" % t)
             nc.sync.dma_start(plane[:], x_rows[:, t, :])
             planes.append(plane)
+            if t == 0:
+                nc.sync.dma_start(gate_rows[0:E, :], gate[0, :].rearrange("(e c) -> e c", e=E))
 
         groups = ((0, 2), (2, 6), (6, 12))
         w_src = w_words.rearrange("e a p b -> p (e a) b").bitcast(I32)
@@ -68,11 +69,10 @@ def tile_moe_pre_lin_none_kernel(tc, xT, w_words, w_scales, gate, offs, out):
                 )
             s_tiles.append(s_tile)
 
-        gate_t = bank(5, [P, 3, P])
-        for i in range(3):
-            nc.tensor.transpose(gate_t[:, i, :], gate_rows[:, i * C : (i + 1) * C], ident[:])
-        gate_col = sb.tile([P, 4, 3], F32, name="gate_col")
-        nc.scalar.activation(gate_col[:], gate_t[:, :, 0:4].rearrange("s i j -> s j i"), COPY)
+        gate_t = bank(5, [P, P])
+        nc.tensor.transpose(gate_t[:], gate_rows[:], ident[:])
+        gate_col = sb.tile([P, E], F32, name="gate_col")
+        nc.scalar.activation(gate_col[:], gate_t[:, 0:E], COPY)
 
         gathered = {}
 
@@ -81,25 +81,25 @@ def tile_moe_pre_lin_none_kernel(tc, xT, w_words, w_scales, gate, offs, out):
             nc.vector.tensor_copy(dst, planes[t][:].indirect(slots_list(e0, e1)))
             gathered[group, t] = dst
 
-        def scale_by_gate(group, e):
+        def scale_by_gate(group, e, rounded):
             e0 = groups[group][0]
             turned = bank((0, 1, 2)[e % 3] if e < 6 else (0, 1, 3)[e % 3], [P, PACK, P])
             for t in range(PACK):
                 nc.tensor.transpose(turned[:, t, :], gathered[group, t][:, (e - e0) * C : (e - e0 + 1) * C], ident[:])
-            rounded = sb.tile([P, PACK * P], BF16, name="rounded", bufs=4)
             nc.scalar.activation(
-                rounded[:].rearrange("s (u p h) -> s u p h", u=2, h=2),
+                rounded.rearrange("s (u p h) -> s u p h", u=2, h=2),
                 turned[:].rearrange("s (u h) p -> s u p h", h=2),
                 COPY,
-                scale=gate_col[:, e // 3, e % 3 : e % 3 + 1],
+                scale=gate_col[:, e : e + 1],
             )
-            return rounded
 
         def prepare_pair(group, pair, dst):
             e0 = groups[group][0]
             back = bank((3, 4, 3, 4, 7, 4)[pair], [P, 2, 2, P])
+            rounded = sb.tile([P, 2 * K], BF16, name="rounded%d" % (0, 1, 2, 2, 0, 1)[pair])
             for i in range(2):
-                words = scale_by_gate(group, 2 * pair + i)[:].bitcast(F32)
+                scale_by_gate(group, 2 * pair + i, rounded[:, i * K : (i + 1) * K])
+                words = rounded[:, i * K : (i + 1) * K].bitcast(F32)
                 for u in range(2):
                     nc.tensor.transpose(back[:, i, u, :], words[:, u * P : (u + 1) * P], ident[:])
             first = (2 * pair - e0) * C * 2
@@ -145,41 +145,68 @@ def tile_moe_pre_lin_none_kernel(tc, xT, w_words, w_scales, gate, offs, out):
                         stop=True,
                     )
                 nc.scalar.copy(y[:, (first - e0) * C : (last - e0) * C], acc[:])
-            results[group, b] = y
+            results[group, b] = y[:]
+
+        def multiply_first_rest(index):
+            e0, e1 = groups[0]
+            words, scales = codes[0]
+            width = (e1 - e0) * C
+            y = sb.tile([P, 2 * width], F32, name="y0_rest")
+            acc = bank(index, [P, 2 * width])
+            for b in (1, 2):
+                for e in range(e0, e1):
+                    cols = slice((e - e0) * C, (e - e0 + 1) * C)
+                    w0 = (e - e0) * 2 * N + b * 2 * P
+                    s0 = (e - e0) * N + b * P
+                    first = (b - 1) * width + (e - e0) * C
+                    nc.tensor.matmul_mx(
+                        out=acc[:, first : first + C],
+                        lhsT=w_tiles[0][:, w0 : w0 + 2 * P].bitcast(FP4X4),
+                        lhsT_scale=s_tiles[0][:, s0 : s0 + P],
+                        rhs=words[:, cols].bitcast(FP8X4),
+                        rhs_scale=scales[:, cols],
+                        start=True,
+                        stop=True,
+                    )
+                results[0, b] = y[:, (b - 1) * width : b * width]
+            nc.scalar.copy(y[:], acc[:])
 
         windows = [sb.tile([P, T], F32, name="window%d" % b) for b in range(BLOCKS)]
 
         def scatter(group, b):
             e0, e1 = groups[group]
-            nc.vector.tensor_copy(windows[b][:].indirect(slots_list(e0, e1)), results[group, b][:])
+            nc.vector.tensor_copy(windows[b][:].indirect(slots_list(e0, e1)), results[group, b])
 
         g_a = sb.tile([P, PACK, 2 * C], F32, name="g_a", tag="hold_a", align_bytes=64)
-        g_b = sb.tile([P, PACK, 4 * C], F32, name="g_b")
+        g_b = sb.tile([P, 3, 4 * C], F32, name="g_b")
         g_c0 = sb.tile([P, 6 * C], F32, name="g_c0")
-        for t in range(PACK):
-            gather(0, t, g_a[:, t, :])
-            gather(1, t, g_b[:, t, :])
-            if t == 0:
-                gather(2, 0, g_c0[:])
+        gather(0, 0, g_a[:, 0, :])
+        gather(1, 0, g_b[:, 0, :])
+        gather(2, 0, g_c0[:])
+        gather(0, 1, g_a[:, 1, :])
+        gather(1, 1, g_b[:, 1, :])
+        gather(0, 2, g_a[:, 2, :])
+        gather(0, 3, g_a[:, 3, :])
+        gather(1, 3, g_b[:, 2, :])
 
         q_a = sb.tile([P, 2 * C * PACK], BF16, name="q_a", tag="hold_q", align_bytes=64)
         prepare_pair(0, 0, q_a)
-        g_c12 = sb.tile([P, 2, 6 * C], F32, name="g_c12", tag="hold_a", align_bytes=64)
-        gather(2, 1, g_c12[:, 0, :])
-        gather(2, 2, g_c12[:, 1, :])
+        g_late = sb.tile([P, 16 * C], F32, name="g_late", tag="hold_a", align_bytes=64)
+        gather(1, 2, g_late[:, 0 : 4 * C])
+        gather(2, 1, g_late[:, 4 * C : 10 * C])
+        gather(2, 2, g_late[:, 10 * C : 16 * C])
         quantize(0, q_a)
         g_c3 = sb.tile([P, 6 * C], F32, name="g_c3", tag="hold_q", align_bytes=64)
         gather(2, 3, g_c3[:])
 
         q_b = sb.tile([P, 4 * C * PACK], BF16, name="q_b", align_bytes=64)
         prepare_pair(1, 1, q_b)
-        multiply(0, 0, [0])
+        multiply(0, 0, [5])
         scatter(0, 0)
         prepare_pair(1, 2, q_b)
-        multiply(0, 1, [1])
-        scatter(0, 1)
         quantize(1, q_b)
-        multiply(0, 2, [3])
+        multiply_first_rest(3)
+        scatter(0, 1)
         scatter(0, 2)
         multiply(1, 0, [5])
         multiply(1, 2, [6])

@@ -21,6 +21,8 @@ P = 128
 PACK = 4
 BLOCKS = N // P
 LIST_ROWS = 16
+WIDE = 2048
+PAIRS = ((0, 1), (2, 3), (4, 5), (6, 7), (8, 10), (9, 11))
 
 
 def tile_moe_pre_lin_none_kernel(tc, xT, w_words, w_scales, gate, offs, out):
@@ -46,8 +48,8 @@ def tile_moe_pre_lin_none_kernel(tc, xT, w_words, w_scales, gate, offs, out):
         x_rows = xT.rearrange("(p t) n -> p t n", t=PACK)
         planes = []
         for t in range(PACK):
-            plane = sb.tile([P, T], F32, name="plane%d" % t)
-            nc.sync.dma_start(plane[:], x_rows[:, t, :])
+            plane = sb.tile([P, WIDE if t == 0 else T], F32, name="plane%d" % t)
+            nc.sync.dma_start(plane[:, 0:T], x_rows[:, t, :])
             planes.append(plane)
             if t == 0:
                 nc.sync.dma_start(gate_rows[0:E, :], gate[0, :].rearrange("(e c) -> e c", e=E))
@@ -69,6 +71,8 @@ def tile_moe_pre_lin_none_kernel(tc, xT, w_words, w_scales, gate, offs, out):
                 )
             s_tiles.append(s_tile)
 
+        nc.vector.memset(planes[0][:, T:WIDE], 0.0)
+
         gate_t = bank(5, [P, P])
         nc.tensor.transpose(gate_t[:], gate_rows[:], ident[:])
         gate_col = sb.tile([P, E], F32, name="gate_col")
@@ -76,16 +80,15 @@ def tile_moe_pre_lin_none_kernel(tc, xT, w_words, w_scales, gate, offs, out):
 
         gathered = {}
 
-        def gather(group, t, dst):
-            e0, e1 = groups[group]
+        def gather(t, e0, e1, dst):
             nc.vector.tensor_copy(dst, planes[t][:].indirect(slots_list(e0, e1)))
-            gathered[group, t] = dst
+            for e in range(e0, e1):
+                gathered[e, t] = dst[:, (e - e0) * C : (e - e0 + 1) * C]
 
-        def scale_by_gate(group, e, rounded):
-            e0 = groups[group][0]
-            turned = bank((0, 1, 2)[e % 3] if e < 6 else (0, 1, 3)[e % 3], [P, PACK, P])
+        def scale_by_gate(e, rounded):
+            turned = bank((0, 1, 2, 5, 6, 7, 3, 7, 5, 7, 3, 5)[e], [P, PACK, P])
             for t in range(PACK):
-                nc.tensor.transpose(turned[:, t, :], gathered[group, t][:, (e - e0) * C : (e - e0 + 1) * C], ident[:])
+                nc.tensor.transpose(turned[:, t, :], gathered[e, t], ident[:])
             nc.scalar.activation(
                 rounded.rearrange("s (u p h) -> s u p h", u=2, h=2),
                 turned[:].rearrange("s (u h) p -> s u p h", h=2),
@@ -95,16 +98,17 @@ def tile_moe_pre_lin_none_kernel(tc, xT, w_words, w_scales, gate, offs, out):
 
         def prepare_pair(group, pair, dst):
             e0 = groups[group][0]
-            back = bank((3, 4, 3, 4, 7, 4)[pair], [P, 2, 2, P])
+            back = bank((3, 4, 3, 4, 0, 4)[pair], [P, 2, 2, P])
             rounded = sb.tile([P, 2 * K], BF16, name="rounded%d" % (0, 1, 2, 2, 0, 1)[pair])
             for i in range(2):
-                scale_by_gate(group, 2 * pair + i, rounded[:, i * K : (i + 1) * K])
+                scale_by_gate(PAIRS[pair][i], rounded[:, i * K : (i + 1) * K])
                 words = rounded[:, i * K : (i + 1) * K].bitcast(F32)
                 for u in range(2):
                     nc.tensor.transpose(back[:, i, u, :], words[:, u * P : (u + 1) * P], ident[:])
-            first = (2 * pair - e0) * C * 2
+            first, second = PAIRS[pair]
+            by_expert = dst[:].bitcast(F32).rearrange("p (e s u) -> p e s u", s=C, u=2)
             nc.scalar.copy(
-                dst[:].bitcast(F32)[:, first : first + 4 * C].rearrange("p (i s u) -> p i s u", i=2, u=2),
+                by_expert[:, first - e0 : second - e0 + 1 : second - first],
                 back[:].rearrange("p i u s -> p i s u"),
             )
 
@@ -122,103 +126,79 @@ def tile_moe_pre_lin_none_kernel(tc, xT, w_words, w_scales, gate, offs, out):
                 )
             codes[group] = (words, scales)
 
-        results = {}
-
-        def multiply(group, b, banks):
-            e0, e1 = groups[group]
+        def product(group, e, b, dst):
+            e0 = groups[group][0]
             words, scales = codes[group]
-            y = sb.tile([P, (e1 - e0) * C], F32, name="y%d_%d" % (group, b))
-            for index, first in zip(banks, range(e0, e1, 4)):
-                last = min(first + 4, e1)
-                acc = bank(index, [P, (last - first) * C])
-                for e in range(first, last):
-                    cols = slice((e - e0) * C, (e - e0 + 1) * C)
-                    w0 = (e - e0) * 2 * N + b * 2 * P
-                    s0 = (e - e0) * N + b * P
-                    nc.tensor.matmul_mx(
-                        out=acc[:, (e - first) * C : (e - first + 1) * C],
-                        lhsT=w_tiles[group][:, w0 : w0 + 2 * P].bitcast(FP4X4),
-                        lhsT_scale=s_tiles[group][:, s0 : s0 + P],
-                        rhs=words[:, cols].bitcast(FP8X4),
-                        rhs_scale=scales[:, cols],
-                        start=True,
-                        stop=True,
-                    )
-                nc.scalar.copy(y[:, (first - e0) * C : (last - e0) * C], acc[:])
-            results[group, b] = y[:]
+            cols = slice((e - e0) * C, (e - e0 + 1) * C)
+            w0 = (e - e0) * 2 * N + b * 2 * P
+            s0 = (e - e0) * N + b * P
+            nc.tensor.matmul_mx(
+                out=dst,
+                lhsT=w_tiles[group][:, w0 : w0 + 2 * P].bitcast(FP4X4),
+                lhsT_scale=s_tiles[group][:, s0 : s0 + P],
+                rhs=words[:, cols].bitcast(FP8X4),
+                rhs_scale=scales[:, cols],
+                start=True,
+                stop=True,
+            )
 
-        def multiply_first_rest(index):
-            e0, e1 = groups[0]
-            words, scales = codes[0]
-            width = (e1 - e0) * C
-            y = sb.tile([P, 2 * width], F32, name="y0_rest")
-            acc = bank(index, [P, 2 * width])
-            for b in (1, 2):
-                for e in range(e0, e1):
-                    cols = slice((e - e0) * C, (e - e0 + 1) * C)
-                    w0 = (e - e0) * 2 * N + b * 2 * P
-                    s0 = (e - e0) * N + b * P
-                    first = (b - 1) * width + (e - e0) * C
-                    nc.tensor.matmul_mx(
-                        out=acc[:, first : first + C],
-                        lhsT=w_tiles[0][:, w0 : w0 + 2 * P].bitcast(FP4X4),
-                        lhsT_scale=s_tiles[0][:, s0 : s0 + P],
-                        rhs=words[:, cols].bitcast(FP8X4),
-                        rhs_scale=scales[:, cols],
-                        start=True,
-                        stop=True,
-                    )
-                results[0, b] = y[:, (b - 1) * width : b * width]
-            nc.scalar.copy(y[:], acc[:])
+        def multiply(group, items, index, dst):
+            acc = bank(index, [P, len(items) * C])
+            for i, (e, b) in enumerate(items):
+                product(group, e, b, acc[:, i * C : (i + 1) * C])
+            nc.scalar.copy(dst, acc[:])
 
         windows = [sb.tile([P, T], F32, name="window%d" % b) for b in range(BLOCKS)]
 
-        def scatter(group, b):
-            e0, e1 = groups[group]
-            nc.vector.tensor_copy(windows[b][:].indirect(slots_list(e0, e1)), results[group, b])
+        def scatter(b, e0, e1, src):
+            nc.vector.tensor_copy(windows[b][:].indirect(slots_list(e0, e1)), src)
 
-        g_a = sb.tile([P, PACK, 2 * C], F32, name="g_a", tag="hold_a", align_bytes=64)
-        g_b = sb.tile([P, 3, 4 * C], F32, name="g_b")
-        g_c0 = sb.tile([P, 6 * C], F32, name="g_c0")
-        gather(0, 0, g_a[:, 0, :])
-        gather(1, 0, g_b[:, 0, :])
-        gather(2, 0, g_c0[:])
-        gather(0, 1, g_a[:, 1, :])
-        gather(1, 1, g_b[:, 1, :])
-        gather(0, 2, g_a[:, 2, :])
-        gather(0, 3, g_a[:, 3, :])
-        gather(1, 3, g_b[:, 2, :])
+        g_0 = sb.tile([P, 12 * C], F32, name="g_0")
+        g_1 = sb.tile([P, 6 * C], F32, name="g_1")
+        g_a = sb.tile([P, 4 * C], F32, name="g_a", tag="hold_a", align_bytes=64)
+        g_3 = sb.tile([P, 4 * C], F32, name="g_3")
+        gather(0, 0, 12, g_0[:])
+        gather(1, 0, 6, g_1[:])
+        gather(2, 0, 2, g_a[:, 0 : 2 * C])
+        gather(3, 0, 2, g_a[:, 2 * C : 4 * C])
+        gather(3, 2, 6, g_3[:])
 
         q_a = sb.tile([P, 2 * C * PACK], BF16, name="q_a", tag="hold_q", align_bytes=64)
         prepare_pair(0, 0, q_a)
         g_late = sb.tile([P, 16 * C], F32, name="g_late", tag="hold_a", align_bytes=64)
-        gather(1, 2, g_late[:, 0 : 4 * C])
-        gather(2, 1, g_late[:, 4 * C : 10 * C])
-        gather(2, 2, g_late[:, 10 * C : 16 * C])
+        gather(2, 2, 6, g_late[:, 0 : 4 * C])
+        gather(1, 6, 12, g_late[:, 4 * C : 10 * C])
+        gather(2, 6, 12, g_late[:, 10 * C : 16 * C])
         quantize(0, q_a)
-        g_c3 = sb.tile([P, 6 * C], F32, name="g_c3", tag="hold_q", align_bytes=64)
-        gather(2, 3, g_c3[:])
+        g_last = sb.tile([P, 6 * C], F32, name="g_last", tag="hold_q", align_bytes=64)
+        gather(3, 6, 12, g_last[:])
 
         q_b = sb.tile([P, 4 * C * PACK], BF16, name="q_b", align_bytes=64)
         prepare_pair(1, 1, q_b)
-        multiply(0, 0, [5])
-        scatter(0, 0)
+        y_a0 = sb.tile([P, 2 * C], F32, name="y_a0")
         prepare_pair(1, 2, q_b)
+        multiply(0, [(0, 0), (1, 0)], 6, y_a0[:])
+        scatter(0, 0, 2, y_a0[:])
         quantize(1, q_b)
-        multiply_first_rest(3)
-        scatter(0, 1)
-        scatter(0, 2)
-        multiply(1, 0, [5])
-        multiply(1, 2, [6])
-        scatter(1, 0)
-        scatter(1, 2)
+        y_ab = sb.tile([P, 8 * C], F32, name="y_ab")
+        multiply(0, [(0, 1), (1, 1), (0, 2), (1, 2)], 3, y_ab[:, 0 : 4 * C])
+        scatter(1, 0, 2, y_ab[:, 0 : 2 * C])
+        multiply(1, [(e, 2) for e in range(2, 6)], 7, y_ab[:, 4 * C : 8 * C])
+        scatter(2, 0, 6, y_ab[:, 2 * C : 8 * C])
+        y_b0 = sb.tile([P, 4 * C], F32, name="y_b0")
+        multiply(1, [(e, 0) for e in range(2, 6)], 5, y_b0[:])
+        scatter(0, 2, 6, y_b0[:])
         q_c = sb.tile([P, 6 * C * PACK], BF16, name="q_c", align_bytes=64)
         for pair in range(3, 6):
             prepare_pair(2, pair, q_c)
         quantize(2, q_c)
-        multiply(1, 1, [4])
-        scatter(1, 1)
+        y_b1 = sb.tile([P, 4 * C], F32, name="y_b1")
+        multiply(1, [(e, 1) for e in range(2, 6)], 4, y_b1[:])
+        scatter(1, 2, 6, y_b1[:])
         for b in range(BLOCKS):
-            multiply(2, b, [(2, 5), (6, 7), (0, 1)][b])
-            scatter(2, b)
+            y_c = sb.tile([P, 6 * C], F32, name="y_c%d" % b)
+            first, second = [(0, 1), (2, 6), (3, 7)][b]
+            multiply(2, [(e, b) for e in range(6, 10)], first, y_c[:, 0 : 4 * C])
+            multiply(2, [(e, b) for e in range(10, 12)], second, y_c[:, 4 * C : 6 * C])
+            scatter(b, 6, 12, y_c[:])
             nc.sync.dma_start(out[b * P : (b + 1) * P, :], windows[b][:])

@@ -5,7 +5,7 @@ from concourse.masks import make_identity
 
 K, T, E, C, N = 512, 1536, 12, 128, 384
 FLOPS = 2 * K * N * E * C
-BYTES = 4 * K * T + E * 128 * 2 * N + E * 16 * N + 4 * T + 2 * T * 8 + 4 * N * T
+BYTES = 4 * K * T + E * (K // 2) * N + E * (K // 32) * N + 4 * T + 128 * (T // 16) * 2 + 4 * N * T
 
 F32 = mybir.dt.float32
 BF16 = mybir.dt.bfloat16
@@ -21,8 +21,12 @@ P = 128
 PACK = 4
 BLOCKS = N // P
 LIST_ROWS = 16
+QUADRANT = 32
+QUADRANT_ROWS = 4
+BANK_EXPERTS = 4
+QUANT_WORDS = 512
 WIDE = 2048
-PAIRS = ((0, 1), (2, 3), (4, 5), (6, 7), (8, 10), (9, 11))
+GROUPS = ((0, 2), (2, 6), (6, 12))
 
 
 def tile_moe_pre_lin_none_kernel(tc, xT, w_words, w_scales, gate, offs, out):
@@ -54,29 +58,27 @@ def tile_moe_pre_lin_none_kernel(tc, xT, w_words, w_scales, gate, offs, out):
             if t == 0:
                 nc.sync.dma_start(gate_rows[0:E, :], gate[0, :].rearrange("(e c) -> e c", e=E))
 
-        groups = ((0, 2), (2, 6), (6, 12))
         w_src = w_words.rearrange("e a p b -> p (e a) b").bitcast(I32)
-        s_src = w_scales.rearrange("e a (q r) n -> r q (e a) n", r=4).bitcast(I32)
+        s_src = w_scales.rearrange("e a (q r) n -> r q (e a) n", r=QUADRANT_ROWS).bitcast(I32)
         w_tiles = []
         s_tiles = []
-        for i, (e0, e1) in enumerate(groups):
-            w_tile = sb.tile([P, (e1 - e0) * 2 * N], U8, name="w%d" % i, align_bytes=64)
+        for group, (e0, e1) in enumerate(GROUPS):
+            w_tile = sb.tile([P, (e1 - e0) * 2 * N], U8, name="w%d" % group, align_bytes=64)
             nc.sync.dma_start(w_tile[:].bitcast(I32).rearrange("p (e b) -> p e b", e=e1 - e0), w_src[:, e0:e1, :])
             w_tiles.append(w_tile)
-            s_tile = sb.tile([P, (e1 - e0) * N], U8, name="s%d" % i, align_bytes=64)
+            s_tile = sb.tile([P, (e1 - e0) * N], U8, name="s%d" % group, align_bytes=64)
             nc.vector.memset(s_tile[:].bitcast(I32), 0)
-            for r in range(4):
-                nc.sync.dma_start(
-                    s_tile[:].bitcast(I32).rearrange("p (e n) -> p e n", e=e1 - e0)[r:P:32], s_src[r][:, e0:e1, :]
-                )
+            s_dst = s_tile[:].bitcast(I32).rearrange("p (e n) -> p e n", e=e1 - e0)
+            for r in range(QUADRANT_ROWS):
+                nc.sync.dma_start(s_dst[r:P:QUADRANT], s_src[r][:, e0:e1, :])
             s_tiles.append(s_tile)
 
         nc.vector.memset(planes[0][:, T:WIDE], 0.0)
 
-        gate_t = bank(5, [P, P])
-        nc.tensor.transpose(gate_t[:], gate_rows[:], ident[:])
+        gate_turned = bank(5, [P, P])
+        nc.tensor.transpose(gate_turned[:], gate_rows[:], ident[:])
         gate_col = sb.tile([P, E], F32, name="gate_col")
-        nc.scalar.activation(gate_col[:], gate_t[:, 0:E], COPY)
+        nc.scalar.activation(gate_col[:], gate_turned[:, 0:E], COPY)
 
         gathered = {}
 
@@ -85,120 +87,120 @@ def tile_moe_pre_lin_none_kernel(tc, xT, w_words, w_scales, gate, offs, out):
             for e in range(e0, e1):
                 gathered[e, t] = dst[:, (e - e0) * C : (e - e0 + 1) * C]
 
-        def scale_by_gate(e, rounded):
-            turned = bank((0, 1, 2, 5, 6, 7, 3, 7, 5, 7, 3, 5)[e], [P, PACK, P])
-            for t in range(PACK):
-                nc.tensor.transpose(turned[:, t, :], gathered[e, t], ident[:])
-            nc.scalar.activation(
-                rounded.rearrange("s (u p h) -> s u p h", u=2, h=2),
-                turned[:].rearrange("s (u h) p -> s u p h", h=2),
-                COPY,
-                scale=gate_col[:, e : e + 1],
-            )
-
-        def prepare_pair(group, pair, dst):
-            e0 = groups[group][0]
-            back = bank((3, 4, 3, 4, 0, 4)[pair], [P, 2, 2, P])
-            rounded = sb.tile([P, 2 * K], BF16, name="rounded%d" % (0, 1, 2, 2, 0, 1)[pair])
-            for i in range(2):
-                scale_by_gate(PAIRS[pair][i], rounded[:, i * K : (i + 1) * K])
-                words = rounded[:, i * K : (i + 1) * K].bitcast(F32)
+        def prepare_pair(group, experts, turn_banks, back_bank, dst):
+            back = bank(back_bank, [P, 2, 2, P])
+            rounded = sb.tile([P, 2 * K], BF16, name="rounded%d" % experts[0])
+            for i, e in enumerate(experts):
+                turned = bank(turn_banks[i], [P, PACK, P])
+                for t in range(PACK):
+                    nc.tensor.transpose(turned[:, t, :], gathered[e, t], ident[:])
+                row = rounded[:, i * K : (i + 1) * K]
+                nc.scalar.activation(
+                    row.rearrange("s (u p h) -> s u p h", u=2, h=2),
+                    turned[:].rearrange("s (u h) p -> s u p h", h=2),
+                    COPY,
+                    scale=gate_col[:, e : e + 1],
+                )
+                pair_words = row.bitcast(F32)
                 for u in range(2):
-                    nc.tensor.transpose(back[:, i, u, :], words[:, u * P : (u + 1) * P], ident[:])
-            first, second = PAIRS[pair]
+                    nc.tensor.transpose(back[:, i, u, :], pair_words[:, u * P : (u + 1) * P], ident[:])
+            e0 = GROUPS[group][0]
+            first, second = experts
             by_expert = dst[:].bitcast(F32).rearrange("p (e s u) -> p e s u", s=C, u=2)
             nc.scalar.copy(
                 by_expert[:, first - e0 : second - e0 + 1 : second - first],
                 back[:].rearrange("p i u s -> p i s u"),
             )
 
-        codes = {}
+        quantized = {}
 
         def quantize(group, src):
-            e0, e1 = groups[group]
+            e0, e1 = GROUPS[group]
             width = (e1 - e0) * C
-            words = sb.tile([P, width], U32, name="codes%d" % group, align_bytes=64)
+            codes = sb.tile([P, width], U32, name="codes%d" % group, align_bytes=64)
             scales = sb.tile([P, width], U8, name="scales%d" % group, align_bytes=64)
-            for c0 in range(0, width, 512):
-                c1 = min(c0 + 512, width)
+            for c0 in range(0, width, QUANT_WORDS):
+                c1 = min(c0 + QUANT_WORDS, width)
                 nc.vector.quantize_mx(
-                    out=words[:, c0:c1].bitcast(FP8X4), scales=scales[:, c0:c1], in_=src[:, PACK * c0 : PACK * c1]
+                    out=codes[:, c0:c1].bitcast(FP8X4), scales=scales[:, c0:c1], in_=src[:, PACK * c0 : PACK * c1]
                 )
-            codes[group] = (words, scales)
+            quantized[group] = (codes, scales)
 
-        def product(group, e, b, dst):
-            e0 = groups[group][0]
-            words, scales = codes[group]
-            cols = slice((e - e0) * C, (e - e0 + 1) * C)
-            w0 = (e - e0) * 2 * N + b * 2 * P
-            s0 = (e - e0) * N + b * P
-            nc.tensor.matmul_mx(
-                out=dst,
-                lhsT=w_tiles[group][:, w0 : w0 + 2 * P].bitcast(FP4X4),
-                lhsT_scale=s_tiles[group][:, s0 : s0 + P],
-                rhs=words[:, cols].bitcast(FP8X4),
-                rhs_scale=scales[:, cols],
-                start=True,
-                stop=True,
-            )
-
-        def multiply(group, items, index, dst):
-            acc = bank(index, [P, len(items) * C])
+        def multiply(group, items, acc_bank, dst):
+            e0 = GROUPS[group][0]
+            codes, scales = quantized[group]
+            acc = bank(acc_bank, [P, len(items) * C])
             for i, (e, b) in enumerate(items):
-                product(group, e, b, acc[:, i * C : (i + 1) * C])
+                slots = slice((e - e0) * C, (e - e0 + 1) * C)
+                w0 = (e - e0) * 2 * N + b * 2 * P
+                s0 = (e - e0) * N + b * P
+                nc.tensor.matmul_mx(
+                    out=acc[:, i * C : (i + 1) * C],
+                    lhsT=w_tiles[group][:, w0 : w0 + 2 * P].bitcast(FP4X4),
+                    lhsT_scale=s_tiles[group][:, s0 : s0 + P],
+                    rhs=codes[:, slots].bitcast(FP8X4),
+                    rhs_scale=scales[:, slots],
+                    start=True,
+                    stop=True,
+                )
             nc.scalar.copy(dst, acc[:])
 
         windows = [sb.tile([P, T], F32, name="window%d" % b) for b in range(BLOCKS)]
 
-        def scatter(b, e0, e1, src):
-            nc.vector.tensor_copy(windows[b][:].indirect(slots_list(e0, e1)), src)
+        def scatter(b, group, src):
+            nc.vector.tensor_copy(windows[b][:].indirect(slots_list(*GROUPS[group])), src)
 
-        g_0 = sb.tile([P, 12 * C], F32, name="g_0")
-        g_1 = sb.tile([P, 6 * C], F32, name="g_1")
-        g_a = sb.tile([P, 4 * C], F32, name="g_a", tag="hold_a", align_bytes=64)
-        g_3 = sb.tile([P, 4 * C], F32, name="g_3")
-        gather(0, 0, 12, g_0[:])
-        gather(1, 0, 6, g_1[:])
-        gather(2, 0, 2, g_a[:, 0 : 2 * C])
-        gather(3, 0, 2, g_a[:, 2 * C : 4 * C])
-        gather(3, 2, 6, g_3[:])
+        g_plane0 = sb.tile([P, E * C], F32, name="g_plane0")
+        g_plane1 = sb.tile([P, 6 * C], F32, name="g_plane1")
+        g_first = sb.tile([P, 4 * C], F32, name="g_first", tag="after_group0_turned", align_bytes=64)
+        g_plane3 = sb.tile([P, 4 * C], F32, name="g_plane3")
+        gather(0, 0, 12, g_plane0[:])
+        gather(1, 0, 6, g_plane1[:])
+        gather(2, 0, 2, g_first[:, 0 : 2 * C])
+        gather(3, 0, 2, g_first[:, 2 * C : 4 * C])
+        gather(3, 2, 6, g_plane3[:])
 
-        q_a = sb.tile([P, 2 * C * PACK], BF16, name="q_a", tag="hold_q", align_bytes=64)
-        prepare_pair(0, 0, q_a)
-        g_late = sb.tile([P, 16 * C], F32, name="g_late", tag="hold_a", align_bytes=64)
+        x0 = sb.tile([P, 2 * C * PACK], BF16, name="x0", tag="after_group0_quantized", align_bytes=64)
+        prepare_pair(0, (0, 1), (0, 1), 3, x0)
+
+        g_late = sb.tile([P, 16 * C], F32, name="g_late", tag="after_group0_turned", align_bytes=64)
         gather(2, 2, 6, g_late[:, 0 : 4 * C])
         gather(1, 6, 12, g_late[:, 4 * C : 10 * C])
         gather(2, 6, 12, g_late[:, 10 * C : 16 * C])
-        quantize(0, q_a)
-        g_last = sb.tile([P, 6 * C], F32, name="g_last", tag="hold_q", align_bytes=64)
+        quantize(0, x0)
+        g_last = sb.tile([P, 6 * C], F32, name="g_last", tag="after_group0_quantized", align_bytes=64)
         gather(3, 6, 12, g_last[:])
 
-        q_b = sb.tile([P, 4 * C * PACK], BF16, name="q_b", align_bytes=64)
-        prepare_pair(1, 1, q_b)
-        y_a0 = sb.tile([P, 2 * C], F32, name="y_a0")
-        prepare_pair(1, 2, q_b)
-        multiply(0, [(0, 0), (1, 0)], 6, y_a0[:])
-        scatter(0, 0, 2, y_a0[:])
-        quantize(1, q_b)
-        y_ab = sb.tile([P, 8 * C], F32, name="y_ab")
-        multiply(0, [(0, 1), (1, 1), (0, 2), (1, 2)], 3, y_ab[:, 0 : 4 * C])
-        scatter(1, 0, 2, y_ab[:, 0 : 2 * C])
-        multiply(1, [(e, 2) for e in range(2, 6)], 7, y_ab[:, 4 * C : 8 * C])
-        scatter(2, 0, 6, y_ab[:, 2 * C : 8 * C])
-        y_b0 = sb.tile([P, 4 * C], F32, name="y_b0")
-        multiply(1, [(e, 0) for e in range(2, 6)], 5, y_b0[:])
-        scatter(0, 2, 6, y_b0[:])
-        q_c = sb.tile([P, 6 * C * PACK], BF16, name="q_c", align_bytes=64)
-        for pair in range(3, 6):
-            prepare_pair(2, pair, q_c)
-        quantize(2, q_c)
-        y_b1 = sb.tile([P, 4 * C], F32, name="y_b1")
-        multiply(1, [(e, 1) for e in range(2, 6)], 4, y_b1[:])
-        scatter(1, 2, 6, y_b1[:])
-        for b in range(BLOCKS):
-            y_c = sb.tile([P, 6 * C], F32, name="y_c%d" % b)
-            first, second = [(0, 1), (2, 6), (3, 7)][b]
-            multiply(2, [(e, b) for e in range(6, 10)], first, y_c[:, 0 : 4 * C])
-            multiply(2, [(e, b) for e in range(10, 12)], second, y_c[:, 4 * C : 6 * C])
-            scatter(b, 6, 12, y_c[:])
+        x1 = sb.tile([P, 4 * C * PACK], BF16, name="x1", align_bytes=64)
+        prepare_pair(1, (2, 3), (2, 5), 4, x1)
+        prepare_pair(1, (4, 5), (6, 7), 3, x1)
+        y0_first = sb.tile([P, 2 * C], F32, name="y0_first")
+        multiply(0, [(0, 0), (1, 0)], 6, y0_first[:])
+        scatter(0, 0, y0_first[:])
+        quantize(1, x1)
+        y0_rest = sb.tile([P, 4 * C], F32, name="y0_rest")
+        multiply(0, [(0, 1), (1, 1), (0, 2), (1, 2)], 3, y0_rest[:])
+        scatter(1, 0, y0_rest[:, 0 : 2 * C])
+        scatter(2, 0, y0_rest[:, 2 * C : 4 * C])
+        for b, acc_bank in ((0, 7), (2, 5)):
+            y1 = sb.tile([P, 4 * C], F32, name="y1_%d" % b)
+            multiply(1, [(e, b) for e in range(*GROUPS[1])], acc_bank, y1[:])
+            scatter(b, 1, y1[:])
+
+        x2 = sb.tile([P, 6 * C * PACK], BF16, name="x2", align_bytes=64)
+        prepare_pair(2, (6, 7), (3, 7), 4, x2)
+        prepare_pair(2, (8, 10), (5, 3), 0, x2)
+        prepare_pair(2, (9, 11), (7, 5), 4, x2)
+        quantize(2, x2)
+        y1_last = sb.tile([P, 4 * C], F32, name="y1_last")
+        multiply(1, [(e, 1) for e in range(*GROUPS[1])], 4, y1_last[:])
+        scatter(1, 1, y1_last[:])
+
+        e0, e1 = GROUPS[2]
+        split = e0 + BANK_EXPERTS
+        for b, (bank_a, bank_b) in enumerate(((0, 1), (2, 6), (3, 7))):
+            y2 = sb.tile([P, 6 * C], F32, name="y2_%d" % b)
+            multiply(2, [(e, b) for e in range(e0, split)], bank_a, y2[:, 0 : BANK_EXPERTS * C])
+            multiply(2, [(e, b) for e in range(split, e1)], bank_b, y2[:, BANK_EXPERTS * C : 6 * C])
+            scatter(b, 2, y2[:])
             nc.sync.dma_start(out[b * P : (b + 1) * P, :], windows[b][:])

from contextlib import ExitStack

import concourse.mybir as mybir
from concourse.masks import make_identity

K, T, E, C, N = 512, 1536, 12, 128, 384
FLOPS = 2 * K * N * E * C
BYTES = 4 * K * T + E * (K // 2) * N + E * (K // 32) * N + 4 * T + 128 * (T // 16) * 2 + 4 * N * T

F32 = mybir.dt.float32
BF16 = mybir.dt.bfloat16
I32 = mybir.dt.int32
U32 = mybir.dt.uint32
U16 = mybir.dt.uint16
U8 = mybir.dt.uint8
FP8X4 = mybir.dt.float8_e4m3fn_x4
FP4X4 = mybir.dt.float4_e2m1fn_x4
COPY = mybir.ActivationFunctionType.Copy

P = 128
PACK = 4
BLOCKS = N // P
LIST_ROWS = 16
QUADRANT = 32
QUADRANT_ROWS = 4
BANK_EXPERTS = 4
QUANT_WORDS = 512
WIDE = 2048
GROUPS = ((0, 2), (2, 6), (6, 12))


def tile_moe_pre_lin_none_kernel(tc, xT, w_words, w_scales, gate, offs, out):
    nc = tc.nc
    with ExitStack() as ctx:
        sb = ctx.enter_context(tc.tile_pool(name="sb", bufs=1))
        ps = ctx.enter_context(tc.psum_pool(name="ps", bufs=1))

        def bank(index, shape):
            return ps.tile(shape, F32, name="bank%d" % index)

        gate_rows = sb.tile([P, C], F32, name="gate_rows")
        nc.gpsimd.memset(gate_rows[:], 0.0)
        ident = sb.tile([P, P], F32, name="ident")
        make_identity(nc, ident[:])

        offsets = sb.tile([P, T // LIST_ROWS], U16, name="offsets")
        nc.sync.dma_start(offsets[:], offs)

        def slots_list(e0, e1):
            return offsets[:, e0 * C // LIST_ROWS : e1 * C // LIST_ROWS]

        x_rows = xT.rearrange("(p t) n -> p t n", t=PACK)
        planes = []
        for t in range(PACK):
            plane = sb.tile([P, WIDE if t == 0 else T], F32, name="plane%d" % t)
            nc.sync.dma_start(plane[:, 0:T], x_rows[:, t, :])
            planes.append(plane)
            if t == 0:
                nc.sync.dma_start(gate_rows[0:E, :], gate[0, :].rearrange("(e c) -> e c", e=E))

        w_src = w_words.rearrange("e a p b -> p (e a) b").bitcast(I32)
        s_src = w_scales.rearrange("e a (q r) n -> r q (e a) n", r=QUADRANT_ROWS).bitcast(I32)
        w_tiles = []
        s_tiles = []
        for group, (e0, e1) in enumerate(GROUPS):
            w_tile = sb.tile([P, (e1 - e0) * 2 * N], U8, name="w%d" % group, align_bytes=64)
            nc.sync.dma_start(w_tile[:].bitcast(I32).rearrange("p (e b) -> p e b", e=e1 - e0), w_src[:, e0:e1, :])
            w_tiles.append(w_tile)
            s_tile = sb.tile([P, (e1 - e0) * N], U8, name="s%d" % group, align_bytes=64)
            nc.vector.memset(s_tile[:].bitcast(I32), 0)
            s_dst = s_tile[:].bitcast(I32).rearrange("p (e n) -> p e n", e=e1 - e0)
            for r in range(QUADRANT_ROWS):
                nc.sync.dma_start(s_dst[r:P:QUADRANT], s_src[r][:, e0:e1, :])
            s_tiles.append(s_tile)

        nc.vector.memset(planes[0][:, T:WIDE], 0.0)

        gate_turned = bank(5, [P, P])
        nc.tensor.transpose(gate_turned[:], gate_rows[:], ident[:])
        gate_col = sb.tile([P, E], F32, name="gate_col")
        nc.scalar.activation(gate_col[:], gate_turned[:, 0:E], COPY)

        gathered = {}

        def gather(t, e0, e1, dst):
            nc.vector.tensor_copy(dst, planes[t][:].indirect(slots_list(e0, e1)))
            for e in range(e0, e1):
                gathered[e, t] = dst[:, (e - e0) * C : (e - e0 + 1) * C]

        def prepare_pair(group, experts, turn_banks, back_bank, dst):
            back = bank(back_bank, [P, 2, 2, P])
            rounded = sb.tile([P, 2 * K], BF16, name="rounded%d" % experts[0])
            for i, e in enumerate(experts):
                turned = bank(turn_banks[i], [P, PACK, P])
                for t in range(PACK):
                    nc.tensor.transpose(turned[:, t, :], gathered[e, t], ident[:])
                row = rounded[:, i * K : (i + 1) * K]
                nc.scalar.activation(
                    row.rearrange("s (u p h) -> s u p h", u=2, h=2),
                    turned[:].rearrange("s (u h) p -> s u p h", h=2),
                    COPY,
                    scale=gate_col[:, e : e + 1],
                )
                pair_words = row.bitcast(F32)
                for u in range(2):
                    nc.tensor.transpose(back[:, i, u, :], pair_words[:, u * P : (u + 1) * P], ident[:])
            e0 = GROUPS[group][0]
            first, second = experts
            by_expert = dst[:].bitcast(F32).rearrange("p (e s u) -> p e s u", s=C, u=2)
            nc.scalar.copy(
                by_expert[:, first - e0 : second - e0 + 1 : second - first],
                back[:].rearrange("p i u s -> p i s u"),
            )

        quantized = {}

        def quantize(group, src):
            e0, e1 = GROUPS[group]
            width = (e1 - e0) * C
            codes = sb.tile([P, width], U32, name="codes%d" % group, align_bytes=64)
            scales = sb.tile([P, width], U8, name="scales%d" % group, align_bytes=64)
            for c0 in range(0, width, QUANT_WORDS):
                c1 = min(c0 + QUANT_WORDS, width)
                nc.vector.quantize_mx(
                    out=codes[:, c0:c1].bitcast(FP8X4), scales=scales[:, c0:c1], in_=src[:, PACK * c0 : PACK * c1]
                )
            quantized[group] = (codes, scales)

        def multiply(group, items, acc_bank, dst):
            e0 = GROUPS[group][0]
            codes, scales = quantized[group]
            acc = bank(acc_bank, [P, len(items) * C])
            for i, (e, b) in enumerate(items):
                slots = slice((e - e0) * C, (e - e0 + 1) * C)
                w0 = (e - e0) * 2 * N + b * 2 * P
                s0 = (e - e0) * N + b * P
                nc.tensor.matmul_mx(
                    out=acc[:, i * C : (i + 1) * C],
                    lhsT=w_tiles[group][:, w0 : w0 + 2 * P].bitcast(FP4X4),
                    lhsT_scale=s_tiles[group][:, s0 : s0 + P],
                    rhs=codes[:, slots].bitcast(FP8X4),
                    rhs_scale=scales[:, slots],
                    start=True,
                    stop=True,
                )
            nc.scalar.copy(dst, acc[:])

        windows = [sb.tile([P, T], F32, name="window%d" % b) for b in range(BLOCKS)]

        def scatter(b, group, src):
            nc.vector.tensor_copy(windows[b][:].indirect(slots_list(*GROUPS[group])), src)

        g_plane0 = sb.tile([P, E * C], F32, name="g_plane0")
        g_plane1 = sb.tile([P, 6 * C], F32, name="g_plane1")
        g_first = sb.tile([P, 4 * C], F32, name="g_first", tag="after_group0_turned", align_bytes=64)
        g_plane3 = sb.tile([P, 4 * C], F32, name="g_plane3")
        gather(0, 0, 12, g_plane0[:])
        gather(1, 0, 6, g_plane1[:])
        gather(2, 0, 2, g_first[:, 0 : 2 * C])
        gather(3, 0, 2, g_first[:, 2 * C : 4 * C])
        gather(3, 2, 6, g_plane3[:])

        x0 = sb.tile([P, 2 * C * PACK], BF16, name="x0", tag="after_group0_quantized", align_bytes=64)
        prepare_pair(0, (0, 1), (0, 1), 3, x0)

        g_late = sb.tile([P, 16 * C], F32, name="g_late", tag="after_group0_turned", align_bytes=64)
        gather(2, 2, 6, g_late[:, 0 : 4 * C])
        gather(1, 6, 12, g_late[:, 4 * C : 10 * C])
        gather(2, 6, 12, g_late[:, 10 * C : 16 * C])
        quantize(0, x0)
        g_last = sb.tile([P, 6 * C], F32, name="g_last", tag="after_group0_quantized", align_bytes=64)
        gather(3, 6, 12, g_last[:])

        x1 = sb.tile([P, 4 * C * PACK], BF16, name="x1", align_bytes=64)
        prepare_pair(1, (2, 3), (2, 5), 4, x1)
        prepare_pair(1, (4, 5), (6, 7), 3, x1)
        y0_first = sb.tile([P, 2 * C], F32, name="y0_first")
        multiply(0, [(0, 0), (1, 0)], 6, y0_first[:])
        scatter(0, 0, y0_first[:])
        quantize(1, x1)
        y0_rest = sb.tile([P, 4 * C], F32, name="y0_rest")
        multiply(0, [(0, 1), (1, 1), (0, 2), (1, 2)], 3, y0_rest[:])
        scatter(1, 0, y0_rest[:, 0 : 2 * C])
        scatter(2, 0, y0_rest[:, 2 * C : 4 * C])
        for b, acc_bank in ((0, 7), (2, 5)):
            y1 = sb.tile([P, 4 * C], F32, name="y1_%d" % b)
            multiply(1, [(e, b) for e in range(*GROUPS[1])], acc_bank, y1[:])
            scatter(b, 1, y1[:])

        x2 = sb.tile([P, 6 * C * PACK], BF16, name="x2", align_bytes=64)
        prepare_pair(2, (6, 7), (3, 7), 4, x2)
        prepare_pair(2, (8, 10), (5, 3), 0, x2)
        prepare_pair(2, (9, 11), (7, 5), 4, x2)
        quantize(2, x2)
        y1_last = sb.tile([P, 4 * C], F32, name="y1_last")
        multiply(1, [(e, 1) for e in range(*GROUPS[1])], 4, y1_last[:])
        scatter(1, 1, y1_last[:])

        e0, e1 = GROUPS[2]
        split = e0 + BANK_EXPERTS
        for b, (bank_a, bank_b) in enumerate(((0, 1), (2, 6), (3, 7))):
            y2 = sb.tile([P, 6 * C], F32, name="y2_%d" % b)
            multiply(2, [(e, b) for e in range(e0, split)], bank_a, y2[:, 0 : BANK_EXPERTS * C])
            multiply(2, [(e, b) for e in range(split, e1)], bank_b, y2[:, BANK_EXPERTS * C : 6 * C])
            scatter(b, 2, y2[:])
            nc.sync.dma_start(out[b * P : (b + 1) * P, :], windows[b][:])
